import numpy as np
import ml_dtypes


def mxq(x, axis, fmt="e4m3"):
    dtype, down = {"e4m3": (ml_dtypes.float8_e4m3fn, 7), "e5m2": (ml_dtypes.float8_e5m2, 14)}[fmt]
    v = np.moveaxis(np.asarray(x, np.float32).astype(ml_dtypes.bfloat16).astype(np.float64), axis, -1)
    blocks = v.reshape(v.shape[:-1] + (-1, 32))
    amax = np.abs(blocks).max(-1, keepdims=True)
    byte = np.maximum(np.where(amax > 0, np.frexp(amax)[1] - 1 + 127, 0) - down, 1)
    scale = np.exp2(byte - 127.0)
    codes = (blocks / scale).astype(np.float32).astype(dtype).astype(np.float64)
    return np.moveaxis((codes * scale).reshape(v.shape), -1, axis)


WIDE = False


def mx_kscale(k):
    if not WIDE:
        return np.ones(k)
    levels = np.array([10, -10, 5, -5, 0])
    if k % 512:
        return np.exp2(np.random.permutation(np.resize(levels, k // 32))).repeat(32)
    a = np.empty((k // 512, 16))
    for p in range(k // 512):
        a[p, :8] = np.random.permutation(np.resize(levels, 8))
        for g in range(8):
            far = levels[np.abs(levels - a[p, g]) >= 10]
            a[p, g + 8] = far[np.random.randint(len(far))]
    return np.exp2(a.ravel()).repeat(32)


def f64(x):
    return np.asarray(x).astype(np.float64)


def striped(idx):
    return np.tile(idx.reshape(-1, 16).T, (8, 1)).astype(np.uint16)


def unstriped(offs):
    return offs[:16].T.reshape(-1).astype(np.int64)


E2M1 = np.array([0.0, 0.5, 1.0, 1.5, 2.0, 3.0, 4.0, 6.0, -0.0, -0.5, -1.0, -1.5, -2.0, -3.0, -4.0, -6.0])


def pack_weight(w, fmt):
    k, n = w.shape
    w = f64(np.asarray(w, np.float32).astype(ml_dtypes.bfloat16)).reshape(k // 32, 32, n)
    amax = np.abs(w).max(1)
    if fmt == "e4m3":
        byte = np.frexp(amax)[1] - 1 + 127 - 7
    else:
        mant, ex = np.frexp(amax / 6.0)
        byte = np.where(mant > 0.5, ex, ex - 1) + 127
    byte = np.clip(np.where(amax > 0, byte, 1), 1, 254)
    scaled = (w * np.exp2(127.0 - byte)[:, None, :]).reshape(k, n).astype(np.float32)
    by_word = np.ascontiguousarray(scaled.reshape(k // 512, 128, 4, n).transpose(0, 1, 3, 2))
    if fmt == "e4m3":
        words = by_word.astype(ml_dtypes.float8_e4m3fn).view(np.uint8)
    else:
        c = by_word.astype(ml_dtypes.float4_e2m1fn).view(np.uint8) & 0xF
        words = (c[..., 0::2] | (c[..., 1::2] << 4)).reshape(k // 512, 128, 2 * n)
    return np.ascontiguousarray(words), np.ascontiguousarray(byte.astype(np.uint8).reshape(k // 512, 16, n))


def unpack_weight(words, scales, fmt):
    g, _, n = scales.shape
    words = np.ascontiguousarray(words).reshape(g, 128, n, -1)
    if fmt == "e4m3":
        vals = words.view(ml_dtypes.float8_e4m3fn).astype(np.float64)
    else:
        nib = np.empty((g, 128, n, 4), np.uint8)
        nib[..., 0::2] = words & 0xF
        nib[..., 1::2] = words >> 4
        vals = E2M1[nib]
    vals = vals * np.repeat(np.exp2(scales.astype(np.float64) - 127.0), 8, axis=1)[..., None]
    return vals.transpose(0, 1, 3, 2).reshape(g * 512, n)


def gelu(v):
    return 0.5 * v * (1.0 + np.tanh(np.sqrt(2.0 / np.pi) * (v + 0.044715 * v**3)))


def striped8(idx):
    return np.concatenate([v.reshape(-1, 16).T for v in idx]).astype(np.uint16)


def unstriped8(offs):
    return np.stack([offs[16 * g:16 * g + 16].T.reshape(-1) for g in range(8)]).astype(np.int64)


def heads(h, wgt, idx8):
    r = np.arange(h.shape[0])
    return wgt[r // 4 % 128] * h[r[:, None], idx8[r % 512 // 64]]


def put_heads(h, wgs, idx8, t2):
    r = np.arange(h.shape[0])
    page = np.zeros((h.shape[0], t2))
    page[r[:, None], idx8[r % 512 // 64]] = wgs[r // 4 % 128] * h
    return page


K, H, N, T, S, P, T2 = 1024, 512, 256, 4096, 1024, 1024, 2048

def setup_inputs():
    n = np.random.standard_normal
    s = mx_kscale(K)[:, None]
    u = mx_kscale(H)[:, None]
    d = {}
    d["tab_words"], d["tab_scales"] = pack_weight(n((K, T)) * s, "e4m3")
    d["offs"] = striped(np.random.permutation(T)[:S])
    d["offs2"] = striped8(np.stack([np.random.permutation(T2)[:S] for _ in range(8)]))
    d["offs3"] = striped8(np.stack([np.random.permutation(T2)[:P] for _ in range(8)]))
    d["w1"] = (n((K, H)) / K**0.5 / s * u.T).astype(np.float32)
    d["w2_words"], d["w2_scales"] = pack_weight(1.5 * n((K, H)) / K**0.5 / s, "e2m1")
    d["w3"] = (0.7 * n((K, H)) / K**0.5 / s * u.T).astype(np.float32)
    d["wgs"] = np.repeat(np.random.uniform(0.5, 2.0, (8, S)), 16, axis=0).astype(np.float32)
    d["wgt"] = np.repeat(np.random.uniform(0.5, 2.0, (8, P)), 16, axis=0).astype(np.float32)
    d["base"] = (0.8 * n((H, P)) * u).astype(np.float32)
    d["w4_words"], d["w4_scales"] = pack_weight(1.6 * n((H, H)) / H**0.5 / u, "e4m3")
    d["w5"] = (1.2 * n((H, N)) / H**0.5 / u).astype(np.float32)
    return d

def reference(tab_words, tab_scales, offs, offs2, offs3, w1, w2_words, w2_scales, w3, wgs, wgt, base, w4_words, w4_scales, w5):
    v = unpack_weight(tab_words, tab_scales, "e4m3")[:, unstriped(offs)]
    a = mxq(f64(w1), 0, "e4m3").T @ v
    b = unpack_weight(w2_words, w2_scales, "e2m1").T @ v
    c = mxq(f64(w3), 0, "e4m3").T @ v
    h = a * np.tanh(b) - c
    page = put_heads(h, f64(wgs), unstriped8(offs2), T2)
    x = heads(page, f64(wgt), unstriped8(offs3))
    z = x + f64(base)
    zq = mxq(z, 0, "e4m3")
    e = unpack_weight(w4_words, w4_scales, "e4m3").T @ zq
    q = z * (1.0 / (1.0 + np.exp(-e)))
    qq = mxq(q, 0, "e4m3")
    return mxq(f64(w5), 0, "e4m3").T @ qq

@@ -1,0 +1,347 @@
+from contextlib import ExitStack
+
+import concourse.mybir as mybir
+from concourse.masks import make_identity
+
+F32 = mybir.dt.float32
+BF16 = mybir.dt.bfloat16
+I32 = mybir.dt.int32
+U32 = mybir.dt.uint32
+U16 = mybir.dt.uint16
+U8 = mybir.dt.uint8
+E4M3 = mybir.dt.float8_e4m3fn_x4
+E2M1 = mybir.dt.float4_e2m1fn_x4
+ACT = mybir.ActivationFunctionType
+ALU = mybir.AluOpType
+
+K, H, N, T, S, M, T2 = 1024, 512, 256, 4096, 1024, 1024, 2048
+FLOPS = 2 * (3 * K * H * S + H * H * M + H * N * M)
+
+P = 128
+PACK = 4
+PASSES = K // (P * PACK)
+HALF = 512
+BLOCKS = S // P
+CHUNKS = [(0, 256), (256, 256), (512, 256), (768, 128), (896, 128)]
+
+
+def tile_list_arousal_review_features_kernel(
+    tc, tab_words, tab_scales, offs, offs2, offs3, w1, w2_words, w2_scales, w3, wgs, wgt, base,
+    w4_words, w4_scales, w5, out,
+):
+    nc = tc.nc
+    with ExitStack() as ctx:
+        keep = ctx.enter_context(tc.tile_pool(name="keep", bufs=1))
+        ring = ctx.enter_context(tc.tile_pool(name="ring", bufs=2))
+        psum = ctx.enter_context(tc.psum_pool(name="psum", bufs=1))
+
+        def bank(b, shape):
+            return psum.tile(shape, F32, name="bank%d" % b, tag="bank%d" % b)
+
+        w2_plane = keep.tile([P, PASSES, H], U8, name="w2_plane", align_bytes=64)
+        nc.vector.memset(w2_plane[:].bitcast(I32), 0)
+        tab_rows = keep.tile([P, T], U8, name="tab_rows", align_bytes=64)
+        nc.vector.memset(tab_rows[0:96, :].bitcast(I32), 0)
+        v_plane = [keep.tile([P, S], U8, name="v_plane%d" % a, align_bytes=64) for a in range(PASSES)]
+        for a in range(PASSES):
+            nc.vector.memset(v_plane[a][:].bitcast(I32), 0)
+        w4_plane_raw = keep.tile([P, H], U8, name="w4_plane_raw", align_bytes=64)
+        nc.gpsimd.memset(w4_plane_raw[:].bitcast(I32), 0)
+        ident = keep.tile([P, P], F32, name="ident")
+        make_identity(nc, ident[:])
+        warm = keep.tile([P, 1], F32, name="warm")
+        nc.scalar.activation(out=warm[:], in_=ident[:, 0:1], func=ACT.Sigmoid)
+
+        picks = keep.tile([P, S // 16], U16, name="picks")
+        nc.sync.dma_start(picks[:], offs)
+        nc.sync.dma_start(
+            out=tab_rows[96:128, :].bitcast(I32), in_=tab_scales.rearrange("a q t -> (a q) t").bitcast(I32)
+        )
+        tab = [keep.tile([P, T], I32, name="tab%d" % a, tag="tab%d" % a) for a in range(PASSES)]
+        nc.sync.dma_start(out=tab[0][:], in_=tab_words[0].rearrange("p t i -> p (t i)").bitcast(I32))
+        for q in range(4):
+            nc.sync.dma_start(
+                out=w2_plane[32 * q : 32 * q + 4, :, :].bitcast(I32),
+                in_=w2_scales[:, 4 * q : 4 * q + 4, :].rearrange("a r c -> r a c").bitcast(I32),
+            )
+        w2_codes = keep.tile([P, PASSES, 2 * H], U8, name="w2_codes", align_bytes=64)
+        nc.sync.dma_start(
+            out=w2_codes[:].bitcast(I32), in_=w2_words.rearrange("a p c -> p a c").bitcast(I32)
+        )
+        nc.sync.dma_start(out=tab[1][:], in_=tab_words[1].rearrange("p t i -> p (t i)").bitcast(I32))
+        for q in range(4):
+            nc.gpsimd.dma_start(
+                out=w4_plane_raw[32 * q : 32 * q + 4, :].bitcast(I32),
+                in_=w4_scales[0, 4 * q : 4 * q + 4, :].bitcast(I32),
+            )
+
+        pages = []
+        for n in range(2):
+            page = keep.tile([P, T2], F32, name="page%d" % n)
+            nc.vector.memset(page[:], 0.0)
+            pages.append(page)
+
+        def load_weight(w, a, pieces, tag):
+            raw = keep.tile([P, PACK, H], F32, name=tag, tag=tag, align_bytes=64)
+            rows = w[a * HALF : (a + 1) * HALF, :].rearrange("(p j) c -> p j c", j=PACK)
+            width = H // pieces
+            for n in range(pieces):
+                cols = slice(n * width, (n + 1) * width)
+                nc.sync.dma_start(out=raw[:, :, cols], in_=rows[:, :, cols])
+            return raw
+
+        def deal_weight(raw, copies, tag):
+            woven = keep.tile([P, PACK * H], BF16, name=tag, tag=tag, align_bytes=64)
+            width = P // len(copies)
+            src = raw[:].rearrange("p j (m t) -> p m j t", t=PACK)
+            dst = woven[:].rearrange("p (t m j) -> p m j t", t=PACK, j=PACK)
+            for n, copy in enumerate(copies):
+                copy(out=dst[:, n * width : (n + 1) * width], in_=src[:, n * width : (n + 1) * width])
+            return woven
+
+        def quantise(name, woven, spans):
+            words = woven.shape[1] // PACK
+            codes = keep.tile([P, words], U32, name=name + "_codes", align_bytes=64)
+            plane = keep.tile([P, words], U8, name=name + "_plane", align_bytes=64)
+            for lo, hi in spans:
+                nc.vector.quantize_mx(
+                    out=codes[:, lo:hi].bitcast(E4M3), scales=plane[:, lo:hi], in_=woven[:, PACK * lo : PACK * hi]
+                )
+            return codes, plane
+
+        w1_raw = [load_weight(w1, a, 1, "w1_raw%d" % a) for a in range(PASSES)]
+        places = keep.tile([P, S // 16], U16, name="places")
+        nc.sync.dma_start(places[:], offs2)
+        wgs_sb = [keep.tile([P, HALF], F32, name="wgs%d" % hf) for hf in range(2)]
+        nc.sync.dma_start(out=wgs_sb[0][:], in_=wgs[:, 0:HALF])
+
+        v_rows = keep.tile([P, S], U8, name="v_rows", align_bytes=64)
+        nc.vector.tensor_copy(out=v_rows[:], in_=tab_rows[:].indirect(picks[:]))
+        for a, queue in enumerate((nc.scalar, nc.gpsimd)):
+            for q in range(4):
+                queue.dma_start(
+                    out=v_plane[a][32 * q : 32 * q + 4, :].bitcast(I32),
+                    in_=v_rows[96 + 16 * a + 4 * q : 96 + 16 * a + 4 * q + 4, :].bitcast(I32),
+                )
+        v_codes = [[None, None], [None, None]]
+        for a in range(PASSES):
+            for hf in range(2):
+                codes = keep.tile([P, HALF], U32, name="v%d_%d" % (a, hf), align_bytes=64)
+                nc.vector.tensor_copy(
+                    out=codes[:], in_=tab[a][:].bitcast(U32).indirect(picks[:, 32 * hf : 32 * (hf + 1)])
+                )
+                v_codes[a][hf] = codes
+
+        def epochs(a, blk):
+            lo = (blk % 4) * P
+            return dict(
+                lhsT=v_codes[a][blk // 4][:, lo : lo + P].bitcast(E4M3),
+                lhsT_scale=v_plane[a][:, blk * P : (blk + 1) * P],
+            )
+
+        u_t = []
+        for blk in range(BLOCKS):
+            acc = bank(blk, [P, H])
+            for a in range(PASSES):
+                nc.tensor.matmul_mx(
+                    out=acc[:], rhs=w2_codes[:, a, :].bitcast(E2M1), rhs_scale=w2_plane[:, a, :],
+                    start=(a == 0), stop=(a == PASSES - 1), **epochs(a, blk),
+                )
+            ut = keep.tile([P, PACK, P], F32, name="u_t%d" % blk)
+            nc.scalar.activation(out=ut[:], in_=acc[:].rearrange("j (p i) -> j i p", i=PACK), func=ACT.Tanh)
+            u_t.append(ut)
+
+        w1_q = []
+        for a in range(PASSES):
+            woven = deal_weight(w1_raw[a], [nc.vector.tensor_copy], "woven%d" % a)
+            w1_q.append(quantise("w1_%d" % a, woven, [(0, H)]))
+        w3_raw = [load_weight(w3, 0, 1, "w3_raw0"), load_weight(w3, 1, 2, "w3_raw1")]
+        w4_raw = keep.tile([P, H], I32, name="w4_raw")
+        nc.sync.dma_start(out=w4_raw[:], in_=w4_words[0].rearrange("p c i -> p (c i)").bitcast(I32))
+        nc.sync.dma_start(out=wgs_sb[1][:], in_=wgs[:, HALF:S])
+        order = keep.tile([P, M // 16], U16, name="order")
+        nc.sync.dma_start(order[:], offs3)
+        wgt_sb = keep.tile([P, M], F32, name="wgt_sb")
+        nc.sync.dma_start(out=wgt_sb[:], in_=wgt)
+        base_sb = keep.tile([P, PACK, M], F32, name="base_sb", tag="tab0")
+        nc.sync.dma_start(out=base_sb[:], in_=base.rearrange("(p i) m -> p i m", i=PACK))
+
+        woven30 = deal_weight(w3_raw[0], [nc.scalar.copy], "woven0")
+        for blk in range(BLOCKS):
+            acc = bank(blk, [P, H])
+            for a in range(PASSES):
+                nc.tensor.matmul_mx(
+                    out=acc[:], rhs=w1_q[a][0][:].bitcast(E4M3), rhs_scale=w1_q[a][1][:],
+                    start=(a == 0), stop=(a == PASSES - 1), **epochs(a, blk),
+                )
+            tanh_b = u_t[blk]
+            if blk >= 6:
+                tag = ["w3_raw1", "woven1"][blk - 6]
+                u_t[blk] = keep.tile([P, PACK, P], F32, name="u_late%d" % blk, tag=tag, align_bytes=64)
+            nc.vector.tensor_tensor(
+                out=u_t[blk][:].rearrange("j i p -> j (i p)"), in0=acc[:],
+                in1=tanh_b[:].rearrange("j i p -> j (i p)"), op=ALU.mult,
+            )
+            if blk == 3:
+                w3_q = [quantise("w3_0", woven30, [(0, H)])]
+                woven31 = deal_weight(w3_raw[1], [nc.scalar.copy, nc.vector.tensor_copy], "woven1")
+                w3_q.append(quantise("w3_1", woven31, [(0, P), (P, 2 * P), (2 * P, H)]))
+
+        w5_raw = keep.tile([P, PACK, N], F32, name="w5_raw", tag="w1_raw0", align_bytes=64)
+        nc.sync.dma_start(out=w5_raw[:], in_=w5.rearrange("(p j) n -> p j n", j=PACK))
+
+        h = {}
+        for i in range(PACK):
+            for hf in range(2):
+                acc = bank(0, [P, 4, P])
+                for a in range(PASSES):
+                    for jb in range(4):
+                        nc.tensor.matmul_mx(
+                            out=acc[:, jb, :], rhs=w3_q[a][0][:, i * P : (i + 1) * P].bitcast(E4M3),
+                            rhs_scale=w3_q[a][1][:, i * P : (i + 1) * P],
+                            start=(a == 0 and jb == 0), stop=(a == PASSES - 1 and jb == 3),
+                            **epochs(a, 4 * hf + jb),
+                        )
+                minus_c = ring.tile([P, 4, P], F32, name="minus_c", tag="turned")
+                nc.scalar.activation(out=minus_c[:], in_=acc[:], func=ACT.Copy, scale=-1.0)
+                acc = bank(1 + hf, [P, HALF])
+                for jb in range(4):
+                    nc.tensor.matmul(
+                        out=acc[:, jb * P : (jb + 1) * P], lhsT=u_t[4 * hf + jb][:, i, :], rhs=ident[:],
+                        is_transpose=True, start=(jb == 0), stop=False,
+                    )
+                for jb in range(4):
+                    nc.tensor.matmul(
+                        out=acc[:, jb * P : (jb + 1) * P], lhsT=minus_c[:, jb, :], rhs=ident[:],
+                        is_transpose=True, start=False, stop=(jb == 3),
+                    )
+                h_sb = keep.tile([P, HALF], F32, name="h%d_%d" % (i, hf), tag="h%d" % (2 * i + hf))
+                nc.scalar.copy(out=h_sb[:], in_=acc[:])
+                h[i, hf] = h_sb
+
+        w4_codes = keep.tile([P, PACK, P], I32, name="w4_codes", align_bytes=64)
+        nc.vector.tensor_copy(out=w4_codes[:], in_=w4_raw[:].rearrange("p (m t) -> p t m", t=PACK))
+        w4_plane = keep.tile([P, PACK, P], U8, name="w4_plane", align_bytes=64)
+        nc.vector.tensor_copy(out=w4_plane[:], in_=w4_plane_raw[:].rearrange("p (m t) -> p t m", t=PACK))
+        woven5 = keep.tile([P, PACK * N], BF16, name="woven5", tag="woven0", align_bytes=64)
+        nc.scalar.copy(
+            out=woven5[:].rearrange("p (c e j) -> p c j e", e=4, j=PACK),
+            in_=w5_raw[:].rearrange("p j (c e) -> p c j e", e=4),
+        )
+        w5_codes, w5_plane = quantise("w5", woven5, [(0, N)])
+
+        z = [keep.tile([P, PACK, w], F32, name="z%d" % n) for n, (lo, w) in enumerate(CHUNKS)]
+        z_woven = [
+            keep.tile([P, w * PACK], BF16, name="z_woven%d" % n, tag="z_woven%d" % n, align_bytes=64) for n, (lo, w) in enumerate(CHUNKS)
+        ]
+
+        def weave_pair(n, first):
+            nc.scalar.copy(
+                out=z_woven[n][:].rearrange("p (c e i) -> p c i e", e=4, i=PACK)[:, :, first : first + 2, :],
+                in_=z[n][:, first : first + 2, :].rearrange("p i (c e) -> p c i e", e=4),
+            )
+
+        def put(i):
+            for hf in range(2):
+                nc.vector.tensor_tensor(
+                    out=pages[i % 2][:].indirect(places[:, 32 * hf : 32 * (hf + 1)]),
+                    in0=h[i, hf][:], in1=wgs_sb[hf][:], op=ALU.mult,
+                )
+
+        def fetch(i, x, lo, width):
+            nc.vector.tensor_tensor(
+                out=x, in0=pages[i % 2][:].indirect(order[:, lo // 16 : (lo + width) // 16]),
+                in1=wgt_sb[:, lo : lo + width], op=ALU.mult,
+            )
+
+        for i in range(PACK - 1):
+            put(i)
+            x = keep.tile([P, M], F32, name="x%d" % i)
+            fetch(i, x[:], 0, M)
+            for hf in range(2):
+                acc = bank(2 * hf, [P, 4, P])
+                for step, src in enumerate((base_sb[:, i, :], x[:])):
+                    for mb in range(4):
+                        lo = hf * HALF + mb * P
+                        nc.tensor.matmul(
+                            out=acc[:, mb, :], lhsT=src[:, lo : lo + P], rhs=ident[:], is_transpose=True,
+                            start=(step == 0 and mb == 0), stop=(step == 1 and mb == 3),
+                        )
+                z_t = ring.tile([P, 4, P], F32, name="z_t", tag="turned")
+                nc.scalar.copy(out=z_t[:], in_=acc[:])
+                acc = bank(1 + 2 * hf, [P, HALF])
+                for mb in range(4):
+                    nc.tensor.transpose(acc[:, mb * P : (mb + 1) * P], z_t[:, mb, :], ident[:])
+                for n, (lo, w) in enumerate(CHUNKS):
+                    if lo // HALF == hf:
+                        nc.scalar.copy(out=z[n][:, i, :], in_=acc[:, lo % HALF : lo % HALF + w])
+            if i == 1:
+                for n in range(len(CHUNKS)):
+                    weave_pair(n, 0)
+
+        last = PACK - 1
+        put(last)
+
+        def finish_z(n):
+            lo, w = CHUNKS[n]
+            tag = "z_woven%d" % (n - 2) if n >= 2 else "x_last%d" % n
+            x = keep.tile([P, w], F32, name="x_last%d" % n, tag=tag, align_bytes=64)
+            fetch(last, x[:], lo, w)
+            nc.vector.tensor_tensor(out=z[n][:, last, :], in0=x[:], in1=base_sb[:, last, lo : lo + w], op=ALU.add)
+            weave_pair(n, 2)
+
+        out_rows = out.rearrange("(b p) m -> p b m", p=P)
+        gates = {}
+        q_woven = {}
+
+        def gate(n):
+            lo, w = CHUNKS[n]
+            codes, plane = quantise("zq%d" % n, z_woven[n], [(0, w)])
+            sig = ring.tile([P, PACK, w], F32, name="sig")
+            for pair in range(2):
+                acc = bank(4 + 2 * (n % 2) + pair, [P, 2, w])
+                for t in range(2):
+                    i = 2 * pair + t
+                    nc.tensor.matmul_mx(
+                        out=acc[:, t, :], lhsT=w4_codes[:, i, :].bitcast(E4M3), lhsT_scale=w4_plane[:, i, :],
+                        rhs=codes[:].bitcast(E4M3), rhs_scale=plane[:], start=True, stop=True,
+                    )
+                nc.scalar.activation(out=sig[:, 2 * pair : 2 * pair + 2, :], in_=acc[:], func=ACT.Sigmoid)
+            gates[n] = sig
+
+        def damp(n):
+            lo, w = CHUNKS[n]
+            woven = ring.tile([P, w * PACK], BF16, name="q_woven", align_bytes=64)
+            nc.vector.tensor_tensor(
+                out=woven[:].rearrange("p (c e i) -> p c i e", e=4, i=PACK),
+                in0=z[n][:].rearrange("p i (c e) -> p c i e", e=4),
+                in1=gates[n][:].rearrange("p i (c e) -> p c i e", e=4),
+                op=ALU.mult,
+            )
+            q_woven[n] = woven
+
+        def score(n):
+            lo, w = CHUNKS[n]
+            codes, plane = quantise("qq%d" % n, q_woven[n], [(0, w)])
+            acc = bank(n % 4, [P, 2, w])
+            for b in range(2):
+                nc.tensor.matmul_mx(
+                    out=acc[:, b, :], lhsT=w5_codes[:, b * P : (b + 1) * P].bitcast(E4M3),
+                    lhsT_scale=w5_plane[:, b * P : (b + 1) * P],
+                    rhs=codes[:].bitcast(E4M3), rhs_scale=plane[:], start=True, stop=True,
+                )
+            scores = keep.tile([P, 2, w], F32, name="scores%d" % n, tag="h%d" % n)
+            nc.scalar.copy(out=scores[:], in_=acc[:])
+            nc.sync.dma_start(out=out_rows[:, :, lo : lo + w], in_=scores[:])
+
+        finish_z(0)
+        finish_z(1)
+        for n in range(len(CHUNKS) + 2):
+            if n < len(CHUNKS):
+                gate(n)
+            if n + 2 < len(CHUNKS):
+                finish_z(n + 2)
+            if 1 <= n <= len(CHUNKS):
+                damp(n - 1)
+            if n >= 2:
+                score(n - 2)

@@ -38,13 +38,12 @@ def tile_list_arousal_review_features_kernel(
         def bank(b, shape):
             return psum.tile(shape, F32, name="bank%d" % b, tag="bank%d" % b)
 
+        tab_rows = keep.tile([P, T], U8, name="tab_rows", tag="tab_rows", align_bytes=64)
+        nc.vector.memset(tab_rows[:].bitcast(I32), 0)
         w2_plane = keep.tile([P, PASSES, H], U8, name="w2_plane", align_bytes=64)
         nc.vector.memset(w2_plane[:].bitcast(I32), 0)
-        tab_rows = keep.tile([P, T], U8, name="tab_rows", align_bytes=64)
-        nc.vector.memset(tab_rows[0:96, :].bitcast(I32), 0)
-        v_plane = [keep.tile([P, S], U8, name="v_plane%d" % a, align_bytes=64) for a in range(PASSES)]
-        for a in range(PASSES):
-            nc.vector.memset(v_plane[a][:].bitcast(I32), 0)
+        v_plane1 = keep.tile([P, S], U8, name="v_plane1", align_bytes=64)
+        nc.vector.memset(v_plane1[:].bitcast(I32), 0)
         w4_plane_raw = keep.tile([P, H], U8, name="w4_plane_raw", align_bytes=64)
         nc.gpsimd.memset(w4_plane_raw[:].bitcast(I32), 0)
         ident = keep.tile([P, P], F32, name="ident")
@@ -54,11 +53,22 @@ def tile_list_arousal_review_features_kernel(
 
         picks = keep.tile([P, S // 16], U16, name="picks")
         nc.sync.dma_start(picks[:], offs)
-        nc.sync.dma_start(
-            out=tab_rows[96:128, :].bitcast(I32), in_=tab_scales.rearrange("a q t -> (a q) t").bitcast(I32)
-        )
+        for q in range(4):
+            nc.sync.dma_start(
+                out=tab_rows[32 * q : 32 * q + 4, :].bitcast(I32),
+                in_=tab_scales[0, 4 * q : 4 * q + 4, :].bitcast(I32),
+            )
+        nc.sync.dma_start(out=tab_rows[8:24, :].bitcast(I32), in_=tab_scales[1].bitcast(I32))
         tab = [keep.tile([P, T], I32, name="tab%d" % a, tag="tab%d" % a) for a in range(PASSES)]
-        nc.sync.dma_start(out=tab[0][:], in_=tab_words[0].rearrange("p t i -> p (t i)").bitcast(I32))
+
+        def load_table(a, half):
+            cols = slice(half * T // 2, (half + 1) * T // 2)
+            words = tab_words[a].rearrange("p t i -> p (t i)").bitcast(I32)
+            nc.sync.dma_start(out=tab[a][:, cols], in_=words[:, cols])
+
+        load_table(0, 0)
+        load_table(0, 1)
+        load_table(1, 0)
         for q in range(4):
             nc.sync.dma_start(
                 out=w2_plane[32 * q : 32 * q + 4, :, :].bitcast(I32),
@@ -68,18 +78,7 @@ def tile_list_arousal_review_features_kernel(
         nc.sync.dma_start(
             out=w2_codes[:].bitcast(I32), in_=w2_words.rearrange("a p c -> p a c").bitcast(I32)
         )
-        nc.sync.dma_start(out=tab[1][:], in_=tab_words[1].rearrange("p t i -> p (t i)").bitcast(I32))
-        for q in range(4):
-            nc.gpsimd.dma_start(
-                out=w4_plane_raw[32 * q : 32 * q + 4, :].bitcast(I32),
-                in_=w4_scales[0, 4 * q : 4 * q + 4, :].bitcast(I32),
-            )
-
-        pages = []
-        for n in range(2):
-            page = keep.tile([P, T2], F32, name="page%d" % n)
-            nc.vector.memset(page[:], 0.0)
-            pages.append(page)
+        load_table(1, 1)
 
         def load_weight(w, a, pieces, tag):
             raw = keep.tile([P, PACK, H], F32, name=tag, tag=tag, align_bytes=64)
@@ -99,6 +98,14 @@ def tile_list_arousal_review_features_kernel(
                 copy(out=dst[:, n * width : (n + 1) * width], in_=src[:, n * width : (n + 1) * width])
             return woven
 
+        def weave_weight(raw, copy, tag):
+            woven = keep.tile([P, PACK * raw.shape[2]], BF16, name=tag, tag=tag, align_bytes=64)
+            copy(
+                out=woven[:].rearrange("p (c e j) -> p c j e", e=4, j=PACK),
+                in_=raw[:].rearrange("p j (c e) -> p c j e", e=4),
+            )
+            return woven
+
         def quantise(name, woven, spans):
             words = woven.shape[1] // PACK
             codes = keep.tile([P, words], U32, name=name + "_codes", align_bytes=64)
@@ -112,17 +119,23 @@ def tile_list_arousal_review_features_kernel(
         w1_raw = [load_weight(w1, a, 1, "w1_raw%d" % a) for a in range(PASSES)]
         places = keep.tile([P, S // 16], U16, name="places")
         nc.sync.dma_start(places[:], offs2)
-        wgs_sb = [keep.tile([P, HALF], F32, name="wgs%d" % hf) for hf in range(2)]
-        nc.sync.dma_start(out=wgs_sb[0][:], in_=wgs[:, 0:HALF])
+        wgs_sb = keep.tile([P, S], F32, name="wgs_sb")
+        nc.sync.dma_start(out=wgs_sb[:, 0:HALF], in_=wgs[:, 0:HALF])
 
-        v_rows = keep.tile([P, S], U8, name="v_rows", align_bytes=64)
-        nc.vector.tensor_copy(out=v_rows[:], in_=tab_rows[:].indirect(picks[:]))
-        for a, queue in enumerate((nc.scalar, nc.gpsimd)):
-            for q in range(4):
-                queue.dma_start(
-                    out=v_plane[a][32 * q : 32 * q + 4, :].bitcast(I32),
-                    in_=v_rows[96 + 16 * a + 4 * q : 96 + 16 * a + 4 * q + 4, :].bitcast(I32),
-                )
+        v_plane0 = keep.tile([P, S], U8, name="v_plane0", align_bytes=64)
+        nc.vector.tensor_copy(out=v_plane0[:], in_=tab_rows[:].indirect(picks[:]))
+        for q in range(4):
+            nc.scalar.dma_start(
+                out=v_plane1[32 * q : 32 * q + 4, :].bitcast(I32),
+                in_=v_plane0[8 + 4 * q : 12 + 4 * q, :].bitcast(I32),
+            )
+        v_plane = [v_plane0, v_plane1]
+        pages = [
+            keep.tile([P, T2], F32, name="page0", tag="tab_rows", align_bytes=64),
+            keep.tile([P, T2], F32, name="page1"),
+        ]
+        for page in pages:
+            nc.vector.memset(page[:], 0.0)
         v_codes = [[None, None], [None, None]]
         for a in range(PASSES):
             for hf in range(2):
@@ -153,22 +166,27 @@ def tile_list_arousal_review_features_kernel(
 
         w1_q = []
         for a in range(PASSES):
-            woven = deal_weight(w1_raw[a], [nc.vector.tensor_copy], "woven%d" % a)
+            woven = weave_weight(w1_raw[a], nc.vector.tensor_copy, "woven%d" % a)
             w1_q.append(quantise("w1_%d" % a, woven, [(0, H)]))
         w3_raw = [load_weight(w3, 0, 1, "w3_raw0"), load_weight(w3, 1, 2, "w3_raw1")]
         w4_raw = keep.tile([P, H], I32, name="w4_raw")
         nc.sync.dma_start(out=w4_raw[:], in_=w4_words[0].rearrange("p c i -> p (c i)").bitcast(I32))
-        nc.sync.dma_start(out=wgs_sb[1][:], in_=wgs[:, HALF:S])
+        nc.sync.dma_start(out=wgs_sb[:, HALF:S], in_=wgs[:, HALF:S])
         order = keep.tile([P, M // 16], U16, name="order")
         nc.sync.dma_start(order[:], offs3)
         wgt_sb = keep.tile([P, M], F32, name="wgt_sb")
         nc.sync.dma_start(out=wgt_sb[:], in_=wgt)
+        for q in range(4):
+            nc.sync.dma_start(
+                out=w4_plane_raw[32 * q : 32 * q + 4, :].bitcast(I32),
+                in_=w4_scales[0, 4 * q : 4 * q + 4, :].bitcast(I32),
+            )
         base_sb = keep.tile([P, PACK, M], F32, name="base_sb", tag="tab0")
         nc.sync.dma_start(out=base_sb[:], in_=base.rearrange("(p i) m -> p i m", i=PACK))
 
         woven30 = deal_weight(w3_raw[0], [nc.scalar.copy], "woven0")
         for blk in range(BLOCKS):
-            acc = bank(blk, [P, H])
+            acc = bank(blk % 4, [P, H])
             for a in range(PASSES):
                 nc.tensor.matmul_mx(
                     out=acc[:], rhs=w1_q[a][0][:].bitcast(E4M3), rhs_scale=w1_q[a][1][:],
@@ -179,8 +197,7 @@ def tile_list_arousal_review_features_kernel(
                 tag = ["w3_raw1", "woven1"][blk - 6]
                 u_t[blk] = keep.tile([P, PACK, P], F32, name="u_late%d" % blk, tag=tag, align_bytes=64)
             nc.vector.tensor_tensor(
-                out=u_t[blk][:].rearrange("j i p -> j (i p)"), in0=acc[:],
-                in1=tanh_b[:].rearrange("j i p -> j (i p)"), op=ALU.mult,
+                out=u_t[blk][:], in0=acc[:].rearrange("j (p i) -> j i p", i=PACK), in1=tanh_b[:], op=ALU.mult
             )
             if blk == 3:
                 w3_q = [quantise("w3_0", woven30, [(0, H)])]
@@ -190,10 +207,11 @@ def tile_list_arousal_review_features_kernel(
         w5_raw = keep.tile([P, PACK, N], F32, name="w5_raw", tag="w1_raw0", align_bytes=64)
         nc.sync.dma_start(out=w5_raw[:], in_=w5.rearrange("(p j) n -> p j n", j=PACK))
 
-        h = {}
+        h = []
         for i in range(PACK):
+            h.append(keep.tile([P, S], F32, name="h%d" % i, tag="h%d" % i))
             for hf in range(2):
-                acc = bank(0, [P, 4, P])
+                acc = bank(4, [P, 4, P])
                 for a in range(PASSES):
                     for jb in range(4):
                         nc.tensor.matmul_mx(
@@ -204,7 +222,7 @@ def tile_list_arousal_review_features_kernel(
                         )
                 minus_c = ring.tile([P, 4, P], F32, name="minus_c", tag="turned")
                 nc.scalar.activation(out=minus_c[:], in_=acc[:], func=ACT.Copy, scale=-1.0)
-                acc = bank(1 + hf, [P, HALF])
+                acc = bank(5 + hf, [P, HALF])
                 for jb in range(4):
                     nc.tensor.matmul(
                         out=acc[:, jb * P : (jb + 1) * P], lhsT=u_t[4 * hf + jb][:, i, :], rhs=ident[:],
@@ -215,19 +233,13 @@ def tile_list_arousal_review_features_kernel(
                         out=acc[:, jb * P : (jb + 1) * P], lhsT=minus_c[:, jb, :], rhs=ident[:],
                         is_transpose=True, start=False, stop=(jb == 3),
                     )
-                h_sb = keep.tile([P, HALF], F32, name="h%d_%d" % (i, hf), tag="h%d" % (2 * i + hf))
-                nc.scalar.copy(out=h_sb[:], in_=acc[:])
-                h[i, hf] = h_sb
+                nc.scalar.copy(out=h[i][:, hf * HALF : (hf + 1) * HALF], in_=acc[:])
 
         w4_codes = keep.tile([P, PACK, P], I32, name="w4_codes", align_bytes=64)
         nc.vector.tensor_copy(out=w4_codes[:], in_=w4_raw[:].rearrange("p (m t) -> p t m", t=PACK))
         w4_plane = keep.tile([P, PACK, P], U8, name="w4_plane", align_bytes=64)
         nc.vector.tensor_copy(out=w4_plane[:], in_=w4_plane_raw[:].rearrange("p (m t) -> p t m", t=PACK))
-        woven5 = keep.tile([P, PACK * N], BF16, name="woven5", tag="woven0", align_bytes=64)
-        nc.scalar.copy(
-            out=woven5[:].rearrange("p (c e j) -> p c j e", e=4, j=PACK),
-            in_=w5_raw[:].rearrange("p j (c e) -> p c j e", e=4),
-        )
+        woven5 = weave_weight(w5_raw, nc.scalar.copy, "woven0")
         w5_codes, w5_plane = quantise("w5", woven5, [(0, N)])
 
         z = [keep.tile([P, PACK, w], F32, name="z%d" % n) for n, (lo, w) in enumerate(CHUNKS)]
@@ -242,10 +254,11 @@ def tile_list_arousal_review_features_kernel(
             )
 
         def put(i):
-            for hf in range(2):
+            width = HALF if i == 0 else S
+            for lo in range(0, S, width):
                 nc.vector.tensor_tensor(
-                    out=pages[i % 2][:].indirect(places[:, 32 * hf : 32 * (hf + 1)]),
-                    in0=h[i, hf][:], in1=wgs_sb[hf][:], op=ALU.mult,
+                    out=pages[i % 2][:].indirect(places[:, lo // 16 : (lo + width) // 16]),
+                    in0=h[i][:, lo : lo + width], in1=wgs_sb[:, lo : lo + width], op=ALU.mult,
                 )
 
         def fetch(i, x, lo, width):
@@ -259,7 +272,7 @@ def tile_list_arousal_review_features_kernel(
             x = keep.tile([P, M], F32, name="x%d" % i)
             fetch(i, x[:], 0, M)
             for hf in range(2):
-                acc = bank(2 * hf, [P, 4, P])
+                acc = bank(4 + 2 * hf, [P, 4, P])
                 for step, src in enumerate((base_sb[:, i, :], x[:])):
                     for mb in range(4):
                         lo = hf * HALF + mb * P
@@ -269,7 +282,7 @@ def tile_list_arousal_review_features_kernel(
                         )
                 z_t = ring.tile([P, 4, P], F32, name="z_t", tag="turned")
                 nc.scalar.copy(out=z_t[:], in_=acc[:])
-                acc = bank(1 + 2 * hf, [P, HALF])
+                acc = bank(5 + 2 * hf, [P, HALF])
                 for mb in range(4):
                     nc.tensor.transpose(acc[:, mb * P : (mb + 1) * P], z_t[:, mb, :], ident[:])
                 for n, (lo, w) in enumerate(CHUNKS):
@@ -299,7 +312,7 @@ def tile_list_arousal_review_features_kernel(
             codes, plane = quantise("zq%d" % n, z_woven[n], [(0, w)])
             sig = ring.tile([P, PACK, w], F32, name="sig")
             for pair in range(2):
-                acc = bank(4 + 2 * (n % 2) + pair, [P, 2, w])
+                acc = bank(2 * (n % 2) + pair, [P, 2, w])
                 for t in range(2):
                     i = 2 * pair + t
                     nc.tensor.matmul_mx(
@@ -323,14 +336,14 @@ def tile_list_arousal_review_features_kernel(
         def score(n):
             lo, w = CHUNKS[n]
             codes, plane = quantise("qq%d" % n, q_woven[n], [(0, w)])
-            acc = bank(n % 4, [P, 2, w])
+            acc = bank(4 + n % 4, [P, 2, w])
             for b in range(2):
                 nc.tensor.matmul_mx(
                     out=acc[:, b, :], lhsT=w5_codes[:, b * P : (b + 1) * P].bitcast(E4M3),
                     lhsT_scale=w5_plane[:, b * P : (b + 1) * P],
                     rhs=codes[:].bitcast(E4M3), rhs_scale=plane[:], start=True, stop=True,
                 )
-            scores = keep.tile([P, 2, w], F32, name="scores%d" % n, tag="h%d" % n)
+            scores = keep.tile([P, 2, w], F32, name="scores%d" % n, tag="h%d" % (n % PACK))
             nc.scalar.copy(out=scores[:], in_=acc[:])
             nc.sync.dma_start(out=out_rows[:, :, lo : lo + w], in_=scores[:])
 

@@ -59,7 +59,7 @@ def tile_list_arousal_review_features_kernel(
                 in_=tab_scales[0, 4 * q : 4 * q + 4, :].bitcast(I32),
             )
         nc.sync.dma_start(out=tab_rows[8:24, :].bitcast(I32), in_=tab_scales[1].bitcast(I32))
-        tab = [keep.tile([P, T], I32, name="tab%d" % a, tag="tab%d" % a) for a in range(PASSES)]
+        tab = [keep.tile([P, T], I32, name="tab%d" % a, tag="tab%d" % a, align_bytes=64) for a in range(PASSES)]
 
         def load_table(a, half):
             cols = slice(half * T // 2, (half + 1) * T // 2)
@@ -89,21 +89,13 @@ def tile_list_arousal_review_features_kernel(
                 nc.sync.dma_start(out=raw[:, :, cols], in_=rows[:, :, cols])
             return raw
 
-        def deal_weight(raw, copies, tag):
-            woven = keep.tile([P, PACK * H], BF16, name=tag, tag=tag, align_bytes=64)
-            width = P // len(copies)
-            src = raw[:].rearrange("p j (m t) -> p m j t", t=PACK)
-            dst = woven[:].rearrange("p (t m j) -> p m j t", t=PACK, j=PACK)
-            for n, copy in enumerate(copies):
-                copy(out=dst[:, n * width : (n + 1) * width], in_=src[:, n * width : (n + 1) * width])
-            return woven
-
-        def weave_weight(raw, copy, tag):
+        def weave_weight(raw, copies, tag):
             woven = keep.tile([P, PACK * raw.shape[2]], BF16, name=tag, tag=tag, align_bytes=64)
-            copy(
-                out=woven[:].rearrange("p (c e j) -> p c j e", e=4, j=PACK),
-                in_=raw[:].rearrange("p j (c e) -> p c j e", e=4),
-            )
+            dst = woven[:].rearrange("p (c e j) -> p c j e", e=4, j=PACK)
+            src = raw[:].rearrange("p j (c e) -> p c j e", e=4)
+            share = raw.shape[2] // 4 // len(copies)
+            for n, copy in enumerate(copies):
+                copy(out=dst[:, n * share : (n + 1) * share], in_=src[:, n * share : (n + 1) * share])
             return woven
 
         def quantise(name, woven, spans):
@@ -166,7 +158,7 @@ def tile_list_arousal_review_features_kernel(
 
         w1_q = []
         for a in range(PASSES):
-            woven = weave_weight(w1_raw[a], nc.vector.tensor_copy, "woven%d" % a)
+            woven = weave_weight(w1_raw[a], [nc.vector.tensor_copy], "woven%d" % a)
             w1_q.append(quantise("w1_%d" % a, woven, [(0, H)]))
         w3_raw = [load_weight(w3, 0, 1, "w3_raw0"), load_weight(w3, 1, 2, "w3_raw1")]
         w4_raw = keep.tile([P, H], I32, name="w4_raw")
@@ -181,10 +173,10 @@ def tile_list_arousal_review_features_kernel(
                 out=w4_plane_raw[32 * q : 32 * q + 4, :].bitcast(I32),
                 in_=w4_scales[0, 4 * q : 4 * q + 4, :].bitcast(I32),
             )
-        base_sb = keep.tile([P, PACK, M], F32, name="base_sb", tag="tab0")
+        base_sb = keep.tile([P, PACK, M], F32, name="base_sb", tag="tab0", align_bytes=64)
         nc.sync.dma_start(out=base_sb[:], in_=base.rearrange("(p i) m -> p i m", i=PACK))
 
-        woven30 = deal_weight(w3_raw[0], [nc.scalar.copy], "woven0")
+        woven30 = weave_weight(w3_raw[0], [nc.scalar.copy], "woven0")
         for blk in range(BLOCKS):
             acc = bank(blk % 4, [P, H])
             for a in range(PASSES):
@@ -201,45 +193,68 @@ def tile_list_arousal_review_features_kernel(
             )
             if blk == 3:
                 w3_q = [quantise("w3_0", woven30, [(0, H)])]
-                woven31 = deal_weight(w3_raw[1], [nc.scalar.copy, nc.vector.tensor_copy], "woven1")
-                w3_q.append(quantise("w3_1", woven31, [(0, P), (P, 2 * P), (2 * P, H)]))
+                woven31 = weave_weight(w3_raw[1], [nc.scalar.copy, nc.vector.tensor_copy], "woven1")
+                w3_q.append(quantise("w3_1", woven31, [(0, H // 2), (H // 2, H)]))
 
         w5_raw = keep.tile([P, PACK, N], F32, name="w5_raw", tag="w1_raw0", align_bytes=64)
         nc.sync.dma_start(out=w5_raw[:], in_=w5.rearrange("(p j) n -> p j n", j=PACK))
 
-        h = []
-        for i in range(PACK):
-            h.append(keep.tile([P, S], F32, name="h%d" % i, tag="h%d" % i))
-            for hf in range(2):
-                acc = bank(4, [P, 4, P])
-                for a in range(PASSES):
-                    for jb in range(4):
-                        nc.tensor.matmul_mx(
-                            out=acc[:, jb, :], rhs=w3_q[a][0][:, i * P : (i + 1) * P].bitcast(E4M3),
-                            rhs_scale=w3_q[a][1][:, i * P : (i + 1) * P],
-                            start=(a == 0 and jb == 0), stop=(a == PASSES - 1 and jb == 3),
-                            **epochs(a, 4 * hf + jb),
-                        )
-                minus_c = ring.tile([P, 4, P], F32, name="minus_c", tag="turned")
-                nc.scalar.activation(out=minus_c[:], in_=acc[:], func=ACT.Copy, scale=-1.0)
-                acc = bank(5 + hf, [P, HALF])
-                for jb in range(4):
-                    nc.tensor.matmul(
-                        out=acc[:, jb * P : (jb + 1) * P], lhsT=u_t[4 * hf + jb][:, i, :], rhs=ident[:],
-                        is_transpose=True, start=(jb == 0), stop=False,
-                    )
-                for jb in range(4):
-                    nc.tensor.matmul(
-                        out=acc[:, jb * P : (jb + 1) * P], lhsT=minus_c[:, jb, :], rhs=ident[:],
-                        is_transpose=True, start=False, stop=(jb == 3),
-                    )
-                nc.scalar.copy(out=h[i][:, hf * HALF : (hf + 1) * HALF], in_=acc[:])
+        minus_c = [
+            keep.tile([P, 4, PACK, P], F32, name="minus_c%d" % hf, tag=tag, align_bytes=64)
+            for hf, tag in enumerate(("w1_raw1", "tab1"))
+        ]
+        h = [keep.tile([P, S], F32, name="h%d" % i, tag="h%d" % i) for i in range(PACK)]
+        c_acc = {}
+
+        def third_product(blk, b):
+            acc = bank(b, [P, H])
+            spans = [(0, 0, H), (1, 0, H // 2), (1, H // 2, H)]
+            for n, (a, lo, hi) in enumerate(spans):
+                nc.tensor.matmul_mx(
+                    out=acc[:, lo:hi], rhs=w3_q[a][0][:, lo:hi].bitcast(E4M3), rhs_scale=w3_q[a][1][:, lo:hi],
+                    start=(n == 0), stop=(n == len(spans) - 1), **epochs(a, blk),
+                )
+            c_acc[blk] = acc
+
+        def negate_c(blk, first, end):
+            nc.scalar.activation(
+                out=minus_c[blk // 4][:, blk % 4, first:end, :],
+                in_=c_acc[blk][:].rearrange("j (p i) -> j i p", i=PACK)[:, first:end, :],
+                func=ACT.Copy, scale=-1.0,
+            )
+
+        def features(i, hf, b):
+            acc = bank(b, [P, HALF])
+            for jb in range(4):
+                nc.tensor.matmul(
+                    out=acc[:, jb * P : (jb + 1) * P], lhsT=u_t[4 * hf + jb][:, i, :], rhs=ident[:],
+                    is_transpose=True, start=(jb == 0), stop=False,
+                )
+            for jb in range(4):
+                nc.tensor.matmul(
+                    out=acc[:, jb * P : (jb + 1) * P], lhsT=minus_c[hf][:, jb, i, :], rhs=ident[:],
+                    is_transpose=True, start=False, stop=(jb == 3),
+                )
+            nc.scalar.copy(out=h[i][:, hf * HALF : (hf + 1) * HALF], in_=acc[:])
+
+        for blk in range(4):
+            third_product(blk, 4 + blk)
+            negate_c(blk, 0, 1)
+        features(0, 0, 2)
+        for blk in range(4):
+            negate_c(blk, 1, PACK)
+        features(1, 0, 3)
+        for blk, b in zip(range(4, BLOCKS), (0, 1, 4, 5)):
+            third_product(blk, b)
+            negate_c(blk, 0, PACK)
+        for n, (i, hf) in enumerate(((0, 1), (1, 1), (2, 0), (2, 1), (3, 0), (3, 1))):
+            features(i, hf, 2 + n % 2)
 
         w4_codes = keep.tile([P, PACK, P], I32, name="w4_codes", align_bytes=64)
         nc.vector.tensor_copy(out=w4_codes[:], in_=w4_raw[:].rearrange("p (m t) -> p t m", t=PACK))
         w4_plane = keep.tile([P, PACK, P], U8, name="w4_plane", align_bytes=64)
         nc.vector.tensor_copy(out=w4_plane[:], in_=w4_plane_raw[:].rearrange("p (m t) -> p t m", t=PACK))
-        woven5 = weave_weight(w5_raw, nc.scalar.copy, "woven0")
+        woven5 = weave_weight(w5_raw, [nc.scalar.copy], "woven0")
         w5_codes, w5_plane = quantise("w5", woven5, [(0, N)])
 
         z = [keep.tile([P, PACK, w], F32, name="z%d" % n) for n, (lo, w) in enumerate(CHUNKS)]
@@ -253,13 +268,11 @@ def tile_list_arousal_review_features_kernel(
                 in_=z[n][:, first : first + 2, :].rearrange("p i (c e) -> p c i e", e=4),
             )
 
-        def put(i):
-            width = HALF if i == 0 else S
-            for lo in range(0, S, width):
-                nc.vector.tensor_tensor(
-                    out=pages[i % 2][:].indirect(places[:, lo // 16 : (lo + width) // 16]),
-                    in0=h[i][:, lo : lo + width], in1=wgs_sb[:, lo : lo + width], op=ALU.mult,
-                )
+        def put(i, lo, width):
+            nc.vector.tensor_tensor(
+                out=pages[i % 2][:].indirect(places[:, lo // 16 : (lo + width) // 16]),
+                in0=h[i][:, lo : lo + width], in1=wgs_sb[:, lo : lo + width], op=ALU.mult,
+            )
 
         def fetch(i, x, lo, width):
             nc.vector.tensor_tensor(
@@ -267,12 +280,16 @@ def tile_list_arousal_review_features_kernel(
                 in1=wgt_sb[:, lo : lo + width], op=ALU.mult,
             )
 
+        for lo in (0, HALF):
+            for i in range(2):
+                put(i, lo, HALF)
         for i in range(PACK - 1):
-            put(i)
+            if i == 2:
+                put(i, 0, S)
             x = keep.tile([P, M], F32, name="x%d" % i)
             fetch(i, x[:], 0, M)
             for hf in range(2):
-                acc = bank(4 + 2 * hf, [P, 4, P])
+                acc = bank(2 + hf, [P, 4, P])
                 for step, src in enumerate((base_sb[:, i, :], x[:])):
                     for mb in range(4):
                         lo = hf * HALF + mb * P
@@ -282,7 +299,7 @@ def tile_list_arousal_review_features_kernel(
                         )
                 z_t = ring.tile([P, 4, P], F32, name="z_t", tag="turned")
                 nc.scalar.copy(out=z_t[:], in_=acc[:])
-                acc = bank(5 + 2 * hf, [P, HALF])
+                acc = bank(4 + hf, [P, HALF])
                 for mb in range(4):
                     nc.tensor.transpose(acc[:, mb * P : (mb + 1) * P], z_t[:, mb, :], ident[:])
                 for n, (lo, w) in enumerate(CHUNKS):
@@ -293,7 +310,7 @@ def tile_list_arousal_review_features_kernel(
                     weave_pair(n, 0)
 
         last = PACK - 1
-        put(last)
+        put(last, 0, S)
 
         def finish_z(n):
             lo, w = CHUNKS[n]
@@ -312,7 +329,7 @@ def tile_list_arousal_review_features_kernel(
             codes, plane = quantise("zq%d" % n, z_woven[n], [(0, w)])
             sig = ring.tile([P, PACK, w], F32, name="sig")
             for pair in range(2):
-                acc = bank(2 * (n % 2) + pair, [P, 2, w])
+                acc = bank(6 * (n % 2) + pair, [P, 2, w])
                 for t in range(2):
                     i = 2 * pair + t
                     nc.tensor.matmul_mx(
@@ -336,7 +353,7 @@ def tile_list_arousal_review_features_kernel(
         def score(n):
             lo, w = CHUNKS[n]
             codes, plane = quantise("qq%d" % n, q_woven[n], [(0, w)])
-            acc = bank(4 + n % 4, [P, 2, w])
+            acc = bank(2 + n % 4, [P, 2, w])
             for b in range(2):
                 nc.tensor.matmul_mx(
                     out=acc[:, b, :], lhsT=w5_codes[:, b * P : (b + 1) * P].bitcast(E4M3),

from contextlib import ExitStack

import concourse.mybir as mybir
from concourse.masks import make_identity

F32 = mybir.dt.float32
BF16 = mybir.dt.bfloat16
I32 = mybir.dt.int32
U32 = mybir.dt.uint32
U16 = mybir.dt.uint16
U8 = mybir.dt.uint8
E4M3 = mybir.dt.float8_e4m3fn_x4
E2M1 = mybir.dt.float4_e2m1fn_x4
ACT = mybir.ActivationFunctionType
ALU = mybir.AluOpType

K, H, N, T, S, M, T2 = 1024, 512, 256, 4096, 1024, 1024, 2048
FLOPS = 2 * (3 * K * H * S + H * H * M + H * N * M)

P = 128
PACK = 4
PASSES = K // (P * PACK)
HALF = 512
BLOCKS = S // P
CHUNKS = [(0, 256), (256, 256), (512, 256), (768, 128), (896, 128)]


def tile_list_arousal_review_features_kernel(
    tc, tab_words, tab_scales, offs, offs2, offs3, w1, w2_words, w2_scales, w3, wgs, wgt, base,
    w4_words, w4_scales, w5, out,
):
    nc = tc.nc
    with ExitStack() as ctx:
        keep = ctx.enter_context(tc.tile_pool(name="keep", bufs=1))
        ring = ctx.enter_context(tc.tile_pool(name="ring", bufs=2))
        psum = ctx.enter_context(tc.psum_pool(name="psum", bufs=1))

        def bank(b, shape):
            return psum.tile(shape, F32, name="bank%d" % b, tag="bank%d" % b)

        tab_rows = keep.tile([P, T], U8, name="tab_rows", tag="tab_rows", align_bytes=64)
        nc.vector.memset(tab_rows[:].bitcast(I32), 0)
        w2_plane = keep.tile([P, PASSES, H], U8, name="w2_plane", align_bytes=64)
        nc.vector.memset(w2_plane[:].bitcast(I32), 0)
        v_plane1 = keep.tile([P, S], U8, name="v_plane1", align_bytes=64)
        nc.vector.memset(v_plane1[:].bitcast(I32), 0)
        w4_plane_raw = keep.tile([P, H], U8, name="w4_plane_raw", align_bytes=64)
        nc.gpsimd.memset(w4_plane_raw[:].bitcast(I32), 0)
        ident = keep.tile([P, P], F32, name="ident")
        make_identity(nc, ident[:])
        warm = keep.tile([P, 1], F32, name="warm")
        nc.scalar.activation(out=warm[:], in_=ident[:, 0:1], func=ACT.Sigmoid)

        picks = keep.tile([P, S // 16], U16, name="picks")
        nc.sync.dma_start(picks[:], offs)
        for q in range(4):
            nc.sync.dma_start(
                out=tab_rows[32 * q : 32 * q + 4, :].bitcast(I32),
                in_=tab_scales[0, 4 * q : 4 * q + 4, :].bitcast(I32),
            )
        nc.sync.dma_start(out=tab_rows[8:24, :].bitcast(I32), in_=tab_scales[1].bitcast(I32))
        tab = [keep.tile([P, T], I32, name="tab%d" % a, tag="tab%d" % a, align_bytes=64) for a in range(PASSES)]

        def load_table(a, half):
            cols = slice(half * T // 2, (half + 1) * T // 2)
            words = tab_words[a].rearrange("p t i -> p (t i)").bitcast(I32)
            nc.sync.dma_start(out=tab[a][:, cols], in_=words[:, cols])

        load_table(0, 0)
        load_table(0, 1)
        load_table(1, 0)
        for q in range(4):
            nc.sync.dma_start(
                out=w2_plane[32 * q : 32 * q + 4, :, :].bitcast(I32),
                in_=w2_scales[:, 4 * q : 4 * q + 4, :].rearrange("a r c -> r a c").bitcast(I32),
            )
        w2_codes = keep.tile([P, PASSES, 2 * H], U8, name="w2_codes", align_bytes=64)
        nc.sync.dma_start(
            out=w2_codes[:].bitcast(I32), in_=w2_words.rearrange("a p c -> p a c").bitcast(I32)
        )
        load_table(1, 1)

        def load_weight(w, a, pieces, tag):
            raw = keep.tile([P, PACK, H], F32, name=tag, tag=tag, align_bytes=64)
            rows = w[a * HALF : (a + 1) * HALF, :].rearrange("(p j) c -> p j c", j=PACK)
            width = H // pieces
            for n in range(pieces):
                cols = slice(n * width, (n + 1) * width)
                nc.sync.dma_start(out=raw[:, :, cols], in_=rows[:, :, cols])
            return raw

        def weave_weight(raw, copies, tag):
            woven = keep.tile([P, PACK * raw.shape[2]], BF16, name=tag, tag=tag, align_bytes=64)
            dst = woven[:].rearrange("p (c e j) -> p c j e", e=4, j=PACK)
            src = raw[:].rearrange("p j (c e) -> p c j e", e=4)
            share = raw.shape[2] // 4 // len(copies)
            for n, copy in enumerate(copies):
                copy(out=dst[:, n * share : (n + 1) * share], in_=src[:, n * share : (n + 1) * share])
            return woven

        def quantise(name, woven, spans):
            words = woven.shape[1] // PACK
            codes = keep.tile([P, words], U32, name=name + "_codes", align_bytes=64)
            plane = keep.tile([P, words], U8, name=name + "_plane", align_bytes=64)
            for lo, hi in spans:
                nc.vector.quantize_mx(
                    out=codes[:, lo:hi].bitcast(E4M3), scales=plane[:, lo:hi], in_=woven[:, PACK * lo : PACK * hi]
                )
            return codes, plane

        w1_raw = [load_weight(w1, a, 1, "w1_raw%d" % a) for a in range(PASSES)]
        places = keep.tile([P, S // 16], U16, name="places")
        nc.sync.dma_start(places[:], offs2)
        wgs_sb = keep.tile([P, S], F32, name="wgs_sb")
        nc.sync.dma_start(out=wgs_sb[:, 0:HALF], in_=wgs[:, 0:HALF])

        v_plane0 = keep.tile([P, S], U8, name="v_plane0", align_bytes=64)
        nc.vector.tensor_copy(out=v_plane0[:], in_=tab_rows[:].indirect(picks[:]))
        for q in range(4):
            nc.scalar.dma_start(
                out=v_plane1[32 * q : 32 * q + 4, :].bitcast(I32),
                in_=v_plane0[8 + 4 * q : 12 + 4 * q, :].bitcast(I32),
            )
        v_plane = [v_plane0, v_plane1]
        pages = [
            keep.tile([P, T2], F32, name="page0", tag="tab_rows", align_bytes=64),
            keep.tile([P, T2], F32, name="page1"),
        ]
        for page in pages:
            nc.vector.memset(page[:], 0.0)
        v_codes = [[None, None], [None, None]]
        for a in range(PASSES):
            for hf in range(2):
                codes = keep.tile([P, HALF], U32, name="v%d_%d" % (a, hf), align_bytes=64)
                nc.vector.tensor_copy(
                    out=codes[:], in_=tab[a][:].bitcast(U32).indirect(picks[:, 32 * hf : 32 * (hf + 1)])
                )
                v_codes[a][hf] = codes

        def epochs(a, blk):
            lo = (blk % 4) * P
            return dict(
                lhsT=v_codes[a][blk // 4][:, lo : lo + P].bitcast(E4M3),
                lhsT_scale=v_plane[a][:, blk * P : (blk + 1) * P],
            )

        u_t = []
        for blk in range(BLOCKS):
            acc = bank(blk, [P, H])
            for a in range(PASSES):
                nc.tensor.matmul_mx(
                    out=acc[:], rhs=w2_codes[:, a, :].bitcast(E2M1), rhs_scale=w2_plane[:, a, :],
                    start=(a == 0), stop=(a == PASSES - 1), **epochs(a, blk),
                )
            ut = keep.tile([P, PACK, P], F32, name="u_t%d" % blk)
            nc.scalar.activation(out=ut[:], in_=acc[:].rearrange("j (p i) -> j i p", i=PACK), func=ACT.Tanh)
            u_t.append(ut)

        w1_q = []
        for a in range(PASSES):
            woven = weave_weight(w1_raw[a], [nc.vector.tensor_copy], "woven%d" % a)
            w1_q.append(quantise("w1_%d" % a, woven, [(0, H)]))
        w3_raw = [load_weight(w3, 0, 1, "w3_raw0"), load_weight(w3, 1, 2, "w3_raw1")]
        w4_raw = keep.tile([P, H], I32, name="w4_raw")
        nc.sync.dma_start(out=w4_raw[:], in_=w4_words[0].rearrange("p c i -> p (c i)").bitcast(I32))
        nc.sync.dma_start(out=wgs_sb[:, HALF:S], in_=wgs[:, HALF:S])
        order = keep.tile([P, M // 16], U16, name="order")
        nc.sync.dma_start(order[:], offs3)
        wgt_sb = keep.tile([P, M], F32, name="wgt_sb")
        nc.sync.dma_start(out=wgt_sb[:], in_=wgt)
        for q in range(4):
            nc.sync.dma_start(
                out=w4_plane_raw[32 * q : 32 * q + 4, :].bitcast(I32),
                in_=w4_scales[0, 4 * q : 4 * q + 4, :].bitcast(I32),
            )
        base_sb = keep.tile([P, PACK, M], F32, name="base_sb", tag="tab0", align_bytes=64)
        nc.sync.dma_start(out=base_sb[:], in_=base.rearrange("(p i) m -> p i m", i=PACK))

        woven30 = weave_weight(w3_raw[0], [nc.scalar.copy], "woven0")
        for blk in range(BLOCKS):
            acc = bank(blk % 4, [P, H])
            for a in range(PASSES):
                nc.tensor.matmul_mx(
                    out=acc[:], rhs=w1_q[a][0][:].bitcast(E4M3), rhs_scale=w1_q[a][1][:],
                    start=(a == 0), stop=(a == PASSES - 1), **epochs(a, blk),
                )
            tanh_b = u_t[blk]
            if blk >= 6:
                tag = ["w3_raw1", "woven1"][blk - 6]
                u_t[blk] = keep.tile([P, PACK, P], F32, name="u_late%d" % blk, tag=tag, align_bytes=64)
            nc.vector.tensor_tensor(
                out=u_t[blk][:], in0=acc[:].rearrange("j (p i) -> j i p", i=PACK), in1=tanh_b[:], op=ALU.mult
            )
            if blk == 3:
                w3_q = [quantise("w3_0", woven30, [(0, H)])]
                woven31 = weave_weight(w3_raw[1], [nc.scalar.copy, nc.vector.tensor_copy], "woven1")
                w3_q.append(quantise("w3_1", woven31, [(0, H // 2), (H // 2, H)]))

        w5_raw = keep.tile([P, PACK, N], F32, name="w5_raw", tag="w1_raw0", align_bytes=64)
        nc.sync.dma_start(out=w5_raw[:], in_=w5.rearrange("(p j) n -> p j n", j=PACK))

        minus_c = [
            keep.tile([P, 4, PACK, P], F32, name="minus_c%d" % hf, tag=tag, align_bytes=64)
            for hf, tag in enumerate(("w1_raw1", "tab1"))
        ]
        h = [keep.tile([P, S], F32, name="h%d" % i, tag="h%d" % i) for i in range(PACK)]
        c_acc = {}

        def third_product(blk, b):
            acc = bank(b, [P, H])
            spans = [(0, 0, H), (1, 0, H // 2), (1, H // 2, H)]
            for n, (a, lo, hi) in enumerate(spans):
                nc.tensor.matmul_mx(
                    out=acc[:, lo:hi], rhs=w3_q[a][0][:, lo:hi].bitcast(E4M3), rhs_scale=w3_q[a][1][:, lo:hi],
                    start=(n == 0), stop=(n == len(spans) - 1), **epochs(a, blk),
                )
            c_acc[blk] = acc

        def negate_c(blk, first, end):
            nc.scalar.activation(
                out=minus_c[blk // 4][:, blk % 4, first:end, :],
                in_=c_acc[blk][:].rearrange("j (p i) -> j i p", i=PACK)[:, first:end, :],
                func=ACT.Copy, scale=-1.0,
            )

        def features(i, hf, b):
            acc = bank(b, [P, HALF])
            for jb in range(4):
                nc.tensor.matmul(
                    out=acc[:, jb * P : (jb + 1) * P], lhsT=u_t[4 * hf + jb][:, i, :], rhs=ident[:],
                    is_transpose=True, start=(jb == 0), stop=False,
                )
            for jb in range(4):
                nc.tensor.matmul(
                    out=acc[:, jb * P : (jb + 1) * P], lhsT=minus_c[hf][:, jb, i, :], rhs=ident[:],
                    is_transpose=True, start=False, stop=(jb == 3),
                )
            nc.scalar.copy(out=h[i][:, hf * HALF : (hf + 1) * HALF], in_=acc[:])

        for blk in range(4):
            third_product(blk, 4 + blk)
            negate_c(blk, 0, 1)
        features(0, 0, 2)
        for blk in range(4):
            negate_c(blk, 1, PACK)
        features(1, 0, 3)
        for blk, b in zip(range(4, BLOCKS), (0, 1, 4, 5)):
            third_product(blk, b)
            negate_c(blk, 0, PACK)
        for n, (i, hf) in enumerate(((0, 1), (1, 1), (2, 0), (2, 1), (3, 0), (3, 1))):
            features(i, hf, 2 + n % 2)

        w4_codes = keep.tile([P, PACK, P], I32, name="w4_codes", align_bytes=64)
        nc.vector.tensor_copy(out=w4_codes[:], in_=w4_raw[:].rearrange("p (m t) -> p t m", t=PACK))
        w4_plane = keep.tile([P, PACK, P], U8, name="w4_plane", align_bytes=64)
        nc.vector.tensor_copy(out=w4_plane[:], in_=w4_plane_raw[:].rearrange("p (m t) -> p t m", t=PACK))
        woven5 = weave_weight(w5_raw, [nc.scalar.copy], "woven0")
        w5_codes, w5_plane = quantise("w5", woven5, [(0, N)])

        z = [keep.tile([P, PACK, w], F32, name="z%d" % n) for n, (lo, w) in enumerate(CHUNKS)]
        z_woven = [
            keep.tile([P, w * PACK], BF16, name="z_woven%d" % n, tag="z_woven%d" % n, align_bytes=64) for n, (lo, w) in enumerate(CHUNKS)
        ]

        def weave_pair(n, first):
            nc.scalar.copy(
                out=z_woven[n][:].rearrange("p (c e i) -> p c i e", e=4, i=PACK)[:, :, first : first + 2, :],
                in_=z[n][:, first : first + 2, :].rearrange("p i (c e) -> p c i e", e=4),
            )

        def put(i, lo, width):
            nc.vector.tensor_tensor(
                out=pages[i % 2][:].indirect(places[:, lo // 16 : (lo + width) // 16]),
                in0=h[i][:, lo : lo + width], in1=wgs_sb[:, lo : lo + width], op=ALU.mult,
            )

        def fetch(i, x, lo, width):
            nc.vector.tensor_tensor(
                out=x, in0=pages[i % 2][:].indirect(order[:, lo // 16 : (lo + width) // 16]),
                in1=wgt_sb[:, lo : lo + width], op=ALU.mult,
            )

        for lo in (0, HALF):
            for i in range(2):
                put(i, lo, HALF)
        for i in range(PACK - 1):
            if i == 2:
                put(i, 0, S)
            x = keep.tile([P, M], F32, name="x%d" % i)
            fetch(i, x[:], 0, M)
            for hf in range(2):
                acc = bank(2 + hf, [P, 4, P])
                for step, src in enumerate((base_sb[:, i, :], x[:])):
                    for mb in range(4):
                        lo = hf * HALF + mb * P
                        nc.tensor.matmul(
                            out=acc[:, mb, :], lhsT=src[:, lo : lo + P], rhs=ident[:], is_transpose=True,
                            start=(step == 0 and mb == 0), stop=(step == 1 and mb == 3),
                        )
                z_t = ring.tile([P, 4, P], F32, name="z_t", tag="turned")
                nc.scalar.copy(out=z_t[:], in_=acc[:])
                acc = bank(4 + hf, [P, HALF])
                for mb in range(4):
                    nc.tensor.transpose(acc[:, mb * P : (mb + 1) * P], z_t[:, mb, :], ident[:])
                for n, (lo, w) in enumerate(CHUNKS):
                    if lo // HALF == hf:
                        nc.scalar.copy(out=z[n][:, i, :], in_=acc[:, lo % HALF : lo % HALF + w])
            if i == 1:
                for n in range(len(CHUNKS)):
                    weave_pair(n, 0)

        last = PACK - 1
        put(last, 0, S)

        def finish_z(n):
            lo, w = CHUNKS[n]
            tag = "z_woven%d" % (n - 2) if n >= 2 else "x_last%d" % n
            x = keep.tile([P, w], F32, name="x_last%d" % n, tag=tag, align_bytes=64)
            fetch(last, x[:], lo, w)
            nc.vector.tensor_tensor(out=z[n][:, last, :], in0=x[:], in1=base_sb[:, last, lo : lo + w], op=ALU.add)
            weave_pair(n, 2)

        out_rows = out.rearrange("(b p) m -> p b m", p=P)
        gates = {}
        q_woven = {}

        def gate(n):
            lo, w = CHUNKS[n]
            codes, plane = quantise("zq%d" % n, z_woven[n], [(0, w)])
            sig = ring.tile([P, PACK, w], F32, name="sig")
            for pair in range(2):
                acc = bank(6 * (n % 2) + pair, [P, 2, w])
                for t in range(2):
                    i = 2 * pair + t
                    nc.tensor.matmul_mx(
                        out=acc[:, t, :], lhsT=w4_codes[:, i, :].bitcast(E4M3), lhsT_scale=w4_plane[:, i, :],
                        rhs=codes[:].bitcast(E4M3), rhs_scale=plane[:], start=True, stop=True,
                    )
                nc.scalar.activation(out=sig[:, 2 * pair : 2 * pair + 2, :], in_=acc[:], func=ACT.Sigmoid)
            gates[n] = sig

        def damp(n):
            lo, w = CHUNKS[n]
            woven = ring.tile([P, w * PACK], BF16, name="q_woven", align_bytes=64)
            nc.vector.tensor_tensor(
                out=woven[:].rearrange("p (c e i) -> p c i e", e=4, i=PACK),
                in0=z[n][:].rearrange("p i (c e) -> p c i e", e=4),
                in1=gates[n][:].rearrange("p i (c e) -> p c i e", e=4),
                op=ALU.mult,
            )
            q_woven[n] = woven

        def score(n):
            lo, w = CHUNKS[n]
            codes, plane = quantise("qq%d" % n, q_woven[n], [(0, w)])
            acc = bank(2 + n % 4, [P, 2, w])
            for b in range(2):
                nc.tensor.matmul_mx(
                    out=acc[:, b, :], lhsT=w5_codes[:, b * P : (b + 1) * P].bitcast(E4M3),
                    lhsT_scale=w5_plane[:, b * P : (b + 1) * P],
                    rhs=codes[:].bitcast(E4M3), rhs_scale=plane[:], start=True, stop=True,
                )
            scores = keep.tile([P, 2, w], F32, name="scores%d" % n, tag="h%d" % (n % PACK))
            nc.scalar.copy(out=scores[:], in_=acc[:])
            nc.sync.dma_start(out=out_rows[:, :, lo : lo + w], in_=scores[:])

        finish_z(0)
        finish_z(1)
        for n in range(len(CHUNKS) + 2):
            if n < len(CHUNKS):
                gate(n)
            if n + 2 < len(CHUNKS):
                finish_z(n + 2)
            if 1 <= n <= len(CHUNKS):
                damp(n - 1)
            if n >= 2:
                score(n - 2)
